import numpy as np
CORES = [176,177,178,179,180,181,182,183,184,185,186,187,188,189,190,191,48,49,50,51,52,53,54,55,56,57,58,59,60,61,62,63]
N = 32
ROOT = 16
WIDTHS = [1,2,1,1,4,2,4,2,4,1,2,2,1,1,2,4,1,4,1,2,2,4,1,1,2,1,1,2,1,2,4,1]
XW = 4
def setup_inputs(rng):
    return {"x": rng.standard_normal((N, 128, XW), dtype=np.float32)}
def reference(x):
    g = np.concatenate([x[r][:, :WIDTHS[r]] for r in range(N)], axis=1)
    y = np.full((N, 128, g.shape[1]), np.nan, x.dtype)
    y[ROOT] = g
    return {"y": y}

@@ -1,0 +1,104 @@
+import comms_topo
+
+XW_MAX = 4
+TOTAL = 64
+
+SCRATCH = {
+    "stage": ("sbuf", [128, XW_MAX], "float32"),
+    "land": ("sbuf", [128, TOTAL], "float32"),
+}
+SEMAPHORES = ["loaded", "left", "arrived", "stored"]
+
+
+def _place(c):
+    return (comms_topo.host(c), comms_topo.chip(c))
+
+
+def _links(src, dst):
+    d = comms_topo.die(src)
+    h, c = _place(src)
+    out = []
+    if (c ^ comms_topo.chip(dst)) & 1:
+        out.append(("mate", h, c, d))
+        c ^= 1
+    if (h, c) != _place(dst):
+        out.append(("sw_out", h, c, d))
+        out.append(("sw_in",) + _place(dst) + (d,))
+    return out
+
+
+def _plan(cores, widths, root):
+    chips = []
+    for c in cores:
+        if _place(c) not in chips:
+            chips.append(_place(c))
+    load = {}
+    leader_of = {}
+    for p in chips:
+        if p == _place(root):
+            continue
+        members = [c for c in cores if _place(c) == p]
+        cols = sum(widths[cores.index(c)] for c in members)
+        best = None
+        for c in members:
+            if not comms_topo.may_write(c, root):
+                continue
+            worst = max(load.get(k, 0) for k in _links(c, root))
+            key = (worst, comms_topo.die(c) != comms_topo.die(root), -widths[cores.index(c)], c)
+            if best is None or key < best:
+                best = key
+        leader_of[p] = best[-1]
+        for k in _links(best[-1], root):
+            load[k] = load.get(k, 0) + cols
+    return leader_of
+
+
+def _engines(m):
+    return bin(m).count("1")
+
+
+def _load_own(g, T, lo, w):
+    if w == 1:
+        return g.dma_start(T.land[:, lo:lo + 1], T.x[:, 0:1], allow_slow_non_contiguous=True)
+    return g.dma_start(T.land[:, lo:lo + w], T.x[:, 0:w])
+
+
+def rank_program(g, core, T, topo):
+    rank = T.rank_of(core)
+    if rank is None:
+        return
+    cores = list(T.cores)
+    widths = list(T.tables["WIDTHS"])
+    off = [sum(widths[:r]) for r in range(len(widths) + 1)]
+    root = cores[T.root]
+    leader_of = _plan(cores, widths, root)
+    lo, w = off[rank], widths[rank]
+
+    if core == root:
+        _load_own(g, T, lo, w).then_inc(T.sem.loaded, 16)
+        expect = sum(_engines(topo.mask(c, root)) for c in cores if c != root and _place(c) == _place(root))
+        expect += sum(_engines(topo.mask(c, root)) for c in leader_of.values())
+        g.wait_ge(T.sem.arrived, expect)
+        g.wait_ge(T.sem.loaded, 16)
+        g.dma_start(T.y[:, :], T.land[:, 0:off[-1]]).then_inc(T.sem.stored, 16)
+        g.wait_ge(T.sem.stored, 16)
+        return
+
+    leader = leader_of.get(_place(core))
+    if core == leader:
+        members = [c for c in cores if _place(c) == _place(core)]
+        _load_own(g, T, lo, w).then_inc(T.sem.loaded, 16)
+        g.wait_ge(T.sem.arrived, sum(_engines(topo.mask(c, core)) for c in members if c != core))
+        g.wait_ge(T.sem.loaded, 16)
+        b0 = min(off[cores.index(c)] for c in members)
+        b1 = max(off[cores.index(c) + 1] for c in members)
+        src, dst, target = T.land[:, b0:b1], T.land[:, b0:b1], root
+    else:
+        g.dma_start(T.stage[:, :], T.x[:, :]).then_inc(T.sem.loaded, 16)
+        g.wait_ge(T.sem.loaded, 16)
+        src, dst, target = T.stage[:, 0:w], T.land[:, lo:lo + w], (root if leader is None else leader)
+
+    rid, pid = topo.addr(target, core)
+    m = topo.mask(core, target)
+    g.remote_dma(dst, src, T.sem.arrived, T.sem.left, pid, rid, m)
+    g.wait_ge(T.sem.left, _engines(m))

@@ -7,7 +7,7 @@ SCRATCH = {
     "stage": ("sbuf", [128, XW_MAX], "float32"),
     "land": ("sbuf", [128, TOTAL], "float32"),
 }
-SEMAPHORES = ["loaded", "left", "arrived", "stored"]
+SEMAPHORES = ["loaded", "gloaded", "left", "arrived", "stored"]
 
 
 def _place(c):
@@ -59,8 +59,10 @@ def _engines(m):
 
 def _load_own(g, T, lo, w):
     if w == 1:
-        return g.dma_start(T.land[:, lo:lo + 1], T.x[:, 0:1], allow_slow_non_contiguous=True)
-    return g.dma_start(T.land[:, lo:lo + w], T.x[:, 0:w])
+        g.dma_start(T.land[:, lo:lo + 1], T.x[:, 0:1], allow_slow_non_contiguous=True).then_inc(T.sem.gloaded, 16)
+        return T.sem.gloaded
+    g.sync.dma_start(T.land[:, lo:lo + w], T.x[:, 0:w]).then_inc(T.sem.loaded, 16)
+    return T.sem.loaded
 
 
 def rank_program(g, core, T, topo):
@@ -75,26 +77,26 @@ def rank_program(g, core, T, topo):
     lo, w = off[rank], widths[rank]
 
     if core == root:
-        _load_own(g, T, lo, w).then_inc(T.sem.loaded, 16)
+        own = _load_own(g, T, lo, w)
         expect = sum(_engines(topo.mask(c, root)) for c in cores if c != root and _place(c) == _place(root))
         expect += sum(_engines(topo.mask(c, root)) for c in leader_of.values())
-        g.wait_ge(T.sem.arrived, expect)
-        g.wait_ge(T.sem.loaded, 16)
-        g.dma_start(T.y[:, :], T.land[:, 0:off[-1]]).then_inc(T.sem.stored, 16)
-        g.wait_ge(T.sem.stored, 16)
+        g.sync.wait_ge(T.sem.arrived, expect)
+        g.sync.wait_ge(own, 16)
+        g.sync.dma_start(T.y[:, :], T.land[:, 0:off[-1]]).then_inc(T.sem.stored, 16)
+        g.sync.wait_ge(T.sem.stored, 16)
         return
 
     leader = leader_of.get(_place(core))
     if core == leader:
         members = [c for c in cores if _place(c) == _place(core)]
-        _load_own(g, T, lo, w).then_inc(T.sem.loaded, 16)
+        own = _load_own(g, T, lo, w)
         g.wait_ge(T.sem.arrived, sum(_engines(topo.mask(c, core)) for c in members if c != core))
-        g.wait_ge(T.sem.loaded, 16)
+        g.wait_ge(own, 16)
         b0 = min(off[cores.index(c)] for c in members)
         b1 = max(off[cores.index(c) + 1] for c in members)
         src, dst, target = T.land[:, b0:b1], T.land[:, b0:b1], root
     else:
-        g.dma_start(T.stage[:, :], T.x[:, :]).then_inc(T.sem.loaded, 16)
+        g.sync.dma_start(T.stage[:, :], T.x[:, :]).then_inc(T.sem.loaded, 16)
         g.wait_ge(T.sem.loaded, 16)
         src, dst, target = T.stage[:, 0:w], T.land[:, lo:lo + w], (root if leader is None else leader)
 

import comms_topo

XW_MAX = 4
TOTAL = 64

SCRATCH = {
    "stage": ("sbuf", [128, XW_MAX], "float32"),
    "land": ("sbuf", [128, TOTAL], "float32"),
}
SEMAPHORES = ["loaded", "gloaded", "left", "arrived", "stored"]


def _place(c):
    return (comms_topo.host(c), comms_topo.chip(c))


def _links(src, dst):
    d = comms_topo.die(src)
    h, c = _place(src)
    out = []
    if (c ^ comms_topo.chip(dst)) & 1:
        out.append(("mate", h, c, d))
        c ^= 1
    if (h, c) != _place(dst):
        out.append(("sw_out", h, c, d))
        out.append(("sw_in",) + _place(dst) + (d,))
    return out


def _plan(cores, widths, root):
    chips = []
    for c in cores:
        if _place(c) not in chips:
            chips.append(_place(c))
    load = {}
    leader_of = {}
    for p in chips:
        if p == _place(root):
            continue
        members = [c for c in cores if _place(c) == p]
        cols = sum(widths[cores.index(c)] for c in members)
        best = None
        for c in members:
            if not comms_topo.may_write(c, root):
                continue
            worst = max(load.get(k, 0) for k in _links(c, root))
            key = (worst, comms_topo.die(c) != comms_topo.die(root), -widths[cores.index(c)], c)
            if best is None or key < best:
                best = key
        leader_of[p] = best[-1]
        for k in _links(best[-1], root):
            load[k] = load.get(k, 0) + cols
    return leader_of


def _engines(m):
    return bin(m).count("1")


def _load_own(g, T, lo, w):
    if w == 1:
        g.dma_start(T.land[:, lo:lo + 1], T.x[:, 0:1], allow_slow_non_contiguous=True).then_inc(T.sem.gloaded, 16)
        return T.sem.gloaded
    g.sync.dma_start(T.land[:, lo:lo + w], T.x[:, 0:w]).then_inc(T.sem.loaded, 16)
    return T.sem.loaded


def rank_program(g, core, T, topo):
    rank = T.rank_of(core)
    if rank is None:
        return
    cores = list(T.cores)
    widths = list(T.tables["WIDTHS"])
    off = [sum(widths[:r]) for r in range(len(widths) + 1)]
    root = cores[T.root]
    leader_of = _plan(cores, widths, root)
    lo, w = off[rank], widths[rank]

    if core == root:
        own = _load_own(g, T, lo, w)
        expect = sum(_engines(topo.mask(c, root)) for c in cores if c != root and _place(c) == _place(root))
        expect += sum(_engines(topo.mask(c, root)) for c in leader_of.values())
        g.sync.wait_ge(T.sem.arrived, expect)
        g.sync.wait_ge(own, 16)
        g.sync.dma_start(T.y[:, :], T.land[:, 0:off[-1]]).then_inc(T.sem.stored, 16)
        g.sync.wait_ge(T.sem.stored, 16)
        return

    leader = leader_of.get(_place(core))
    if core == leader:
        members = [c for c in cores if _place(c) == _place(core)]
        own = _load_own(g, T, lo, w)
        g.wait_ge(T.sem.arrived, sum(_engines(topo.mask(c, core)) for c in members if c != core))
        g.wait_ge(own, 16)
        b0 = min(off[cores.index(c)] for c in members)
        b1 = max(off[cores.index(c) + 1] for c in members)
        src, dst, target = T.land[:, b0:b1], T.land[:, b0:b1], root
    else:
        g.sync.dma_start(T.stage[:, :], T.x[:, :]).then_inc(T.sem.loaded, 16)
        g.wait_ge(T.sem.loaded, 16)
        src, dst, target = T.stage[:, 0:w], T.land[:, lo:lo + w], (root if leader is None else leader)

    rid, pid = topo.addr(target, core)
    m = topo.mask(core, target)
    g.remote_dma(dst, src, T.sem.arrived, T.sem.left, pid, rid, m)
    g.wait_ge(T.sem.left, _engines(m))
